import numpy as np
import ml_dtypes


def mxq(x, axis, fmt="e4m3"):
    dtype, down = {"e4m3": (ml_dtypes.float8_e4m3fn, 7), "e5m2": (ml_dtypes.float8_e5m2, 14)}[fmt]
    v = np.moveaxis(np.asarray(x, np.float32).astype(ml_dtypes.bfloat16).astype(np.float64), axis, -1)
    blocks = v.reshape(v.shape[:-1] + (-1, 32))
    amax = np.abs(blocks).max(-1, keepdims=True)
    byte = np.maximum(np.where(amax > 0, np.frexp(amax)[1] - 1 + 127, 0) - down, 1)
    scale = np.exp2(byte - 127.0)
    codes = (blocks / scale).astype(np.float32).astype(dtype).astype(np.float64)
    return np.moveaxis((codes * scale).reshape(v.shape), -1, axis)


WIDE = False


def mx_kscale(k):
    if not WIDE:
        return np.ones(k)
    levels = np.array([10, -10, 5, -5, 0])
    if k % 512:
        return np.exp2(np.random.permutation(np.resize(levels, k // 32))).repeat(32)
    a = np.empty((k // 512, 16))
    for p in range(k // 512):
        a[p, :8] = np.random.permutation(np.resize(levels, 8))
        for g in range(8):
            far = levels[np.abs(levels - a[p, g]) >= 10]
            a[p, g + 8] = far[np.random.randint(len(far))]
    return np.exp2(a.ravel()).repeat(32)


def f64(x):
    return np.asarray(x).astype(np.float64)


def striped(idx):
    return np.tile(idx.reshape(-1, 16).T, (8, 1)).astype(np.uint16)


def unstriped(offs):
    return offs[:16].T.reshape(-1).astype(np.int64)


E2M1 = np.array([0.0, 0.5, 1.0, 1.5, 2.0, 3.0, 4.0, 6.0, -0.0, -0.5, -1.0, -1.5, -2.0, -3.0, -4.0, -6.0])


def pack_weight(w, fmt):
    k, n = w.shape
    w = f64(np.asarray(w, np.float32).astype(ml_dtypes.bfloat16)).reshape(k // 32, 32, n)
    amax = np.abs(w).max(1)
    if fmt == "e4m3":
        byte = np.frexp(amax)[1] - 1 + 127 - 7
    else:
        mant, ex = np.frexp(amax / 6.0)
        byte = np.where(mant > 0.5, ex, ex - 1) + 127
    byte = np.clip(np.where(amax > 0, byte, 1), 1, 254)
    scaled = (w * np.exp2(127.0 - byte)[:, None, :]).reshape(k, n).astype(np.float32)
    by_word = np.ascontiguousarray(scaled.reshape(k // 512, 128, 4, n).transpose(0, 1, 3, 2))
    if fmt == "e4m3":
        words = by_word.astype(ml_dtypes.float8_e4m3fn).view(np.uint8)
    else:
        c = by_word.astype(ml_dtypes.float4_e2m1fn).view(np.uint8) & 0xF
        words = (c[..., 0::2] | (c[..., 1::2] << 4)).reshape(k // 512, 128, 2 * n)
    return np.ascontiguousarray(words), np.ascontiguousarray(byte.astype(np.uint8).reshape(k // 512, 16, n))


def unpack_weight(words, scales, fmt):
    g, _, n = scales.shape
    words = np.ascontiguousarray(words).reshape(g, 128, n, -1)
    if fmt == "e4m3":
        vals = words.view(ml_dtypes.float8_e4m3fn).astype(np.float64)
    else:
        nib = np.empty((g, 128, n, 4), np.uint8)
        nib[..., 0::2] = words & 0xF
        nib[..., 1::2] = words >> 4
        vals = E2M1[nib]
    vals = vals * np.repeat(np.exp2(scales.astype(np.float64) - 127.0), 8, axis=1)[..., None]
    return vals.transpose(0, 1, 3, 2).reshape(g * 512, n)


def gelu(v):
    return 0.5 * v * (1.0 + np.tanh(np.sqrt(2.0 / np.pi) * (v + 0.044715 * v**3)))


K, H, N, T, S, T2, P = 1536, 1024, 768, 2048, 512, 1024, 512

def setup_inputs():
    n = np.random.standard_normal
    s = mx_kscale(K)[:, None]
    u = mx_kscale(H)[:, None]
    tab_words, tab_scales = pack_weight(n((K, T)) * s, "e4m3")
    wa4_words, wa4_scales = pack_weight(0.9 * n((K, H)) / np.sqrt(K) / s, "e2m1")
    wo8_words, wo8_scales = pack_weight(n((H, N)) / np.sqrt(H) / u, "e4m3")
    return {
        "tab_words": tab_words, "tab_scales": tab_scales,
        "offs": striped(np.random.permutation(T)[:S]),
        "offs2": striped(np.random.permutation(T2)[:S]),
        "offs3": striped(np.random.permutation(T2)[:P]),
        "wa4_words": wa4_words, "wa4_scales": wa4_scales,
        "wb": (0.5 * n((K, H)) / np.sqrt(K) / s).astype(np.float32),
        "cap": (0.5 * n(H)).astype(np.float32),
        "page0": (0.8 * n((H, T2))).astype(np.float32),
        "wgs": np.exp(0.3 * n((128, S))).astype(np.float32),
        "thr": n(H).astype(np.float32),
        "base": (P * np.random.uniform(0.2, 0.8, H)).astype(np.float32),
        "mat": (2.0 * P * n((H, P)) * u).astype(np.float32),
        "wo8_words": wo8_words, "wo8_scales": wo8_scales,
        "fac": np.exp(0.5 * n((N, P))).astype(np.float32),
    }

def reference(tab_words, tab_scales, offs, offs2, offs3, wa4_words, wa4_scales, wb, cap, page0, wgs, thr, base, mat, wo8_words, wo8_scales, fac):
    v = unpack_weight(tab_words, tab_scales, "e4m3")[:, unstriped(offs)]
    wa = unpack_weight(wa4_words, wa4_scales, "e2m1")
    capped = np.minimum(wa.T @ v, f64(cap)[:, None])
    h = capped + (mxq(f64(wb), 0, "e4m3").T @ v)
    page = f64(page0).copy()
    page[:, unstriped(offs2)] = np.tile(f64(wgs), (H // 128, 1)) * h
    a = 1.0 / (1.0 + np.exp(-(page[:, unstriped(offs3)] + f64(thr)[:, None])))
    y = a / (f64(base)[:, None] + a.sum(axis=1)[:, None]) * f64(mat)
    wo = unpack_weight(wo8_words, wo8_scales, "e4m3")
    return (wo.T @ mxq(y, 0, "e4m3")) * f64(fac)

@@ -1,0 +1,281 @@
+from contextlib import ExitStack
+
+import concourse.mybir as mybir
+from concourse.masks import make_identity
+
+K, H, N, T, S, T2, M = 1536, 1024, 768, 2048, 512, 1024, 512
+FLOPS = 2 * (2 * K * H * S + H * N * M)
+
+F32 = mybir.dt.float32
+BF16 = mybir.dt.bfloat16
+I32 = mybir.dt.int32
+U32 = mybir.dt.uint32
+U16 = mybir.dt.uint16
+U8 = mybir.dt.uint8
+E4M3 = mybir.dt.float8_e4m3fn_x4
+E2M1 = mybir.dt.float4_e2m1fn_x4
+ALU = mybir.AluOpType
+ACT = mybir.ActivationFunctionType
+
+P = 128
+PACK = 4
+K_PASS = P * PACK
+QUADS = 4
+QUAD = P // QUADS
+PASSES = K // K_PASS
+TILES = H // P
+OUT_PASSES = H // K_PASS
+OUT_TILES = N // P
+HALF = S // 2
+CHUNKS = ((0, 1), (1, 1), (2, 2), (4, 2), (6, 2))
+VECTOR_COLS = 320
+PARKED = 6
+
+
+def tile_list_lamp_service_scores_kernel(
+    tc, tab_words, tab_scales, offs, offs2, offs3, wa4_words, wa4_scales, wb, cap, page0, wgs, thr, base, mat,
+    wo8_words, wo8_scales, fac, out,
+):
+    nc = tc.nc
+    with ExitStack() as ctx:
+        lists = ctx.enter_context(tc.tile_pool(name="lists", bufs=1))
+        sb = ctx.enter_context(tc.tile_pool(name="sb", bufs=1))
+        ps = ctx.enter_context(tc.psum_pool(name="ps", bufs=1))
+
+        def new(shape, dtype, name, tag=None):
+            return sb.tile(shape, dtype, name=name, tag=tag or name, align_bytes=64)
+
+        idx = lists.tile([P, S // 16], U16, name="idx")
+        idx2 = lists.tile([P, S // 16], U16, name="idx2")
+        idx3 = lists.tile([P, M // 16], U16, name="idx3")
+
+        tab_sc = new([P, PASSES, T], U8, "tab_sc")
+        wa_sc = new([P, PASSES, H], U8, "wa_sc")
+        wo_sc = new([P, N], U8, "wo_sc")
+        rows = new([P, P], F32, "rows")
+        ident = new([P, P], F32, "ident")
+        nc.vector.memset(tab_sc[:].bitcast(I32), 0)
+        nc.vector.memset(wa_sc[:].bitcast(I32), 0)
+        nc.vector.memset(rows[:], 0.0)
+        nc.vector.memset(wo_sc[:].bitcast(I32), 0)
+        make_identity(nc, ident[:])
+        for src, dst in ((tab_scales, tab_sc), (wa4_scales, wa_sc)):
+            for q in range(QUADS):
+                nc.gpsimd.dma_start(
+                    out=dst[QUAD * q : QUAD * q + 4].bitcast(I32),
+                    in_=src[:, 4 * q : 4 * q + 4, :].rearrange("a r t -> r a t").bitcast(I32),
+                )
+        for j, vec in enumerate((cap, thr, base)):
+            nc.gpsimd.dma_start(out=rows[TILES * j : TILES * (j + 1), :], in_=vec.rearrange("(c p) -> c p", p=P))
+        for q in range(QUADS):
+            nc.gpsimd.dma_start(
+                out=wo_sc[QUAD * q : QUAD * q + 4 * OUT_PASSES, :].bitcast(I32),
+                in_=wo8_scales[:, 4 * q : 4 * q + 4, :].bitcast(I32),
+            )
+
+        tab = [new([P, T], U32, "tab%d" % a) for a in range(PASSES)]
+        wa = [new([P, PASSES, H], U8, "wa%d" % b) for b in range(2)]
+        raw = {}
+        page = [new([P, T2], F32, "page%d" % c) for c in range(TILES)]
+        mat_t = [new([P, M], F32, "mat%d" % c) for c in range(TILES)]
+        fac_t = [new([P, M], F32, "fac%d" % n) for n in range(OUT_TILES)]
+        wgs_t = new([P, S], F32, "wgs")
+        wo = new([P, OUT_PASSES, N], U32, "wo")
+
+        def load_wa(b):
+            nc.sync.dma_start(
+                out=wa[b][:].bitcast(I32),
+                in_=wa4_words[:, :, H * b : H * (b + 1)].rearrange("a p n -> p a n").bitcast(I32),
+            )
+
+        def load_wb(g):
+            first, count = CHUNKS[g]
+            for a in range(PASSES):
+                raw[g, a] = new([P, PACK, P * count], F32, "raw%d_%d" % (g, a))
+                nc.sync.dma_start(
+                    out=raw[g, a][:],
+                    in_=wb[K_PASS * a : K_PASS * (a + 1), P * first : P * (first + count)].rearrange("(p j) c -> p j c", j=PACK),
+                )
+
+        def load_rows(tiles, src, c):
+            nc.sync.dma_start(out=tiles[c][:], in_=src[P * c : P * (c + 1), :])
+
+        nc.sync.dma_start(idx[:], offs)
+        for a in range(PASSES):
+            nc.sync.dma_start(out=tab[a][:].bitcast(I32), in_=tab_words[a].rearrange("p t i -> p (t i)").bitcast(I32))
+        load_wa(0)
+        load_wb(0)
+        load_rows(page, page0, 0)
+        nc.sync.dma_start(out=wgs_t[:], in_=wgs)
+        nc.sync.dma_start(idx2[:], offs2)
+        load_wb(1)
+        load_rows(page, page0, 1)
+        nc.sync.dma_start(idx3[:], offs3)
+        load_wb(2)
+        load_rows(mat_t, mat, 0)
+        load_rows(page, page0, 2)
+        load_rows(mat_t, mat, 1)
+        load_rows(page, page0, 3)
+        load_wa(1)
+        load_wb(3)
+        load_rows(mat_t, mat, 2)
+        load_rows(page, page0, 4)
+        load_rows(mat_t, mat, 3)
+        load_rows(page, page0, 5)
+        load_wb(4)
+        load_rows(mat_t, mat, 4)
+        load_rows(page, page0, 6)
+        nc.sync.dma_start(out=wo[:].bitcast(I32), in_=wo8_words.rearrange("a p c i -> p a (c i)").bitcast(I32))
+        load_rows(mat_t, mat, 5)
+        for n in range(OUT_TILES):
+            load_rows(fac_t, fac, n)
+        load_rows(mat_t, mat, 6)
+        load_rows(mat_t, mat, 7)
+        load_rows(page, page0, 7)
+
+        turned = ps.tile([P, P], F32, name="turned", tag="out0")
+        nc.tensor.transpose(turned[:], rows[:], ident[:])
+        cols = new([P, 3 * TILES], F32, "cols")
+        nc.vector.tensor_copy(out=cols[:], in_=turned[:, : 3 * TILES])
+
+        v_sc = [new([P, S], U8, "v_sc%d" % a) for a in range(PASSES)]
+        v = [new([P, S], U32, "v%d" % a) for a in range(PASSES)]
+        for a in range(PASSES):
+            nc.vector.tensor_copy(out=v_sc[a][:], in_=tab_sc[:, a, :].indirect(idx[:]))
+        for a in range(PASSES):
+            nc.vector.tensor_copy(out=v[a][:], in_=tab[a][:].indirect(idx[:]))
+
+        chunk_of = {first + i: (g, i) for g, (first, count) in enumerate(CHUNKS) for i in range(count)}
+        grouped, wb_q, wb_sc, acc_a, plain, h, x, total, den, y = {}, {}, {}, {}, {}, {}, {}, {}, {}, {}
+        parked = out.bitcast(BF16).rearrange("n (two m) -> (n two) m", two=2)
+        stage, y_q, y_sc, acc = {}, {}, {}, {}
+
+        def interleave(copy, dst, src):
+            copy(out=dst.rearrange("p (c i) t -> p c t i", i=4), in_=src.rearrange("p t (c i) -> p c t i", i=4))
+
+        def round_wb(c):
+            g, i = chunk_of[c]
+            grouped[c] = new([P, PASSES, P, PACK], BF16, "grouped%d" % c)
+            for a in range(PASSES):
+                interleave(nc.scalar.copy, grouped[c][:, a], raw[g, a][:, :, P * i : P * (i + 1)])
+
+        def quantise_wb(c):
+            wb_q[c] = new([P, PASSES * P], U32, "wb_q%d" % c)
+            wb_sc[c] = new([P, PASSES * P], U8, "wb_sc%d" % c)
+            nc.vector.quantize_mx(
+                out=wb_q[c][:].bitcast(E4M3), scales=wb_sc[c][:], in_=grouped[c][:].rearrange("p a c t -> p (a c t)")
+            )
+
+        def products(c):
+            acc_b = ps.tile([P, S], F32, name="acc_b%d" % c, tag="acc_b")
+            for a in range(PASSES):
+                nc.tensor.matmul_mx(
+                    out=acc_b[:], lhsT=wb_q[c][:, P * a : P * (a + 1)].bitcast(E4M3), lhsT_scale=wb_sc[c][:, P * a : P * (a + 1)],
+                    rhs=v[a][:].bitcast(E4M3), rhs_scale=v_sc[a][:], start=a == 0, stop=a == PASSES - 1,
+                )
+            acc_a[c] = ps.tile([P, S], F32, name="acc_a%d" % c, tag="acc_a")
+            b, i = divmod(c, PACK)
+            for a in range(PASSES):
+                nc.tensor.matmul_mx(
+                    out=acc_a[c][:], lhsT=wa[b][:, a, 2 * P * i : 2 * P * (i + 1)].bitcast(E2M1),
+                    lhsT_scale=wa_sc[:, a, P * c : P * (c + 1)],
+                    rhs=v[a][:].bitcast(E4M3), rhs_scale=v_sc[a][:], start=a == 0, stop=a == PASSES - 1,
+                )
+            plain[c] = new([P, S], F32, "plain%d" % c, tag="plain%d" % (c % 2))
+            nc.scalar.copy(out=plain[c][:], in_=acc_b[:])
+
+        def put(c, half):
+            part = slice(HALF * half, HALF * (half + 1))
+            tag = "grouped%d" % (c + 1) if half == 1 and c + 1 < TILES else "h%d" % half
+            h[c, half] = (new([P, HALF], F32, "h%d_%d" % (c, half), tag=tag), tag)
+            nc.vector.scalar_tensor_tensor(
+                out=h[c, half][0][:], in0=acc_a[c][:, part], scalar=cols[:, c : c + 1], in1=plain[c][:, part],
+                op0=ALU.min, op1=ALU.add,
+            )
+            entries = idx2[:, HALF // 16 * half : HALF // 16 * (half + 1)]
+            nc.vector.tensor_tensor(out=page[c][:].indirect(entries), in0=h[c, half][0][:], in1=wgs_t[:, part], op=ALU.mult)
+
+        x_home = ("raw2_2", "raw2_1", "raw3_2", "raw3_1", "raw4_2", "raw4_1", "raw0_2", "raw1_2")
+
+        def look(c):
+            x[c] = new([P, M], F32, "x%d" % c, tag=x_home[c])
+            total[c] = new([P, 1], F32, "total%d" % c)
+            den[c] = new([P, 1], F32, "den%d" % c)
+            nc.scalar.activation(
+                out=x[c][:], in_=page[c][:].indirect(idx3[:]), func=ACT.Sigmoid,
+                bias=cols[:, TILES + c : TILES + c + 1],
+            )
+            nc.scalar.activation(out=x[c][:], in_=x[c][:], func=ACT.Identity, accum_out=total[c][:])
+            nc.scalar.activation(
+                out=den[c][:], in_=total[c][:], func=ACT.Identity, bias=cols[:, 2 * TILES + c : 2 * TILES + c + 1]
+            )
+
+        def weigh(c):
+            tag = h[c + 1, 1][1] if c + 1 < TILES else "rec_last"
+            rec = new([P, 1], F32, "rec%d" % c, tag=tag)
+            nc.vector.reciprocal(out=rec[:], in_=den[c][:])
+            y[c] = new([P, M], BF16, "y%d" % c, tag="y%d" % (c % 2))
+            nc.vector.scalar_tensor_tensor(
+                out=y[c][:], in0=x[c][:], scalar=rec[:], in1=mat_t[c][:], op0=ALU.mult, op1=ALU.mult
+            )
+            b, q = divmod(c, QUADS)
+            if q == 0:
+                stage[b] = new([P, PACK, M], BF16, "stage%d" % b, tag=("raw2_0", "raw4_0")[b])
+            if c >= PARKED:
+                for t in range(PACK):
+                    nc.sync.dma_start(out=stage[b][QUAD * q : QUAD * (q + 1), t, :], in_=y[c][t:P:PACK, :])
+            else:
+                nc.gpsimd.dma_start(out=parked[P * c : P * (c + 1), :], in_=y[c][:])
+                if q == QUADS - 1 or c == PARKED - 1:
+                    nc.gpsimd.dma_start(
+                        out=stage[b][: QUAD * (q + 1)],
+                        in_=parked[K_PASS * b : P * (c + 1), :].rearrange("(p t) m -> p t m", t=PACK),
+                    )
+
+        def quantise_y(b):
+            words = new([P, M, PACK], BF16, "y_words%d" % b, tag=("raw3_0", "raw2_0")[b])
+            if b == 0:
+                interleave(nc.scalar.copy, words[:], stage[b][:])
+            else:
+                interleave(nc.vector.tensor_copy, words[:, :VECTOR_COLS], stage[b][:, :, :VECTOR_COLS])
+                interleave(nc.scalar.copy, words[:, VECTOR_COLS:], stage[b][:, :, VECTOR_COLS:])
+            y_q[b] = new([P, M], U32, "y_q%d" % b)
+            y_sc[b] = new([P, M], U8, "y_sc%d" % b)
+            nc.vector.quantize_mx(out=y_q[b][:].bitcast(E4M3), scales=y_sc[b][:], in_=words[:].rearrange("p m t -> p (m t)"))
+
+        def scores(b, n):
+            if b == 0:
+                acc[n] = ps.tile([P, M], F32, name="acc%d" % n, tag="out%d" % n)
+            nc.tensor.matmul_mx(
+                out=acc[n][:], lhsT=wo[:, b, P * n : P * (n + 1)].bitcast(E4M3), lhsT_scale=wo_sc[4 * b :, P * n : P * (n + 1)],
+                rhs=y_q[b][:].bitcast(E4M3), rhs_scale=y_sc[b][:], start=b == 0, stop=b == OUT_PASSES - 1,
+            )
+
+        round_wb(0)
+        quantise_wb(0)
+        products(0)
+        round_wb(1)
+        for c in range(TILES):
+            put(c, 0)
+            if c + 1 < TILES:
+                quantise_wb(c + 1)
+            put(c, 1)
+            if c + 1 < TILES:
+                products(c + 1)
+            if c % 2 == 0 and c + 3 < TILES:
+                round_wb(c + 2)
+                round_wb(c + 3)
+            look(c)
+            if c >= 1:
+                weigh(c - 1)
+            if c == QUADS + 1:
+                quantise_y(0)
+                for n in range(OUT_TILES):
+                    scores(0, n)
+        weigh(TILES - 1)
+        quantise_y(1)
+        for n in range(OUT_TILES):
+            scores(1, n)
+            result = new([P, M], F32, "result%d" % n, tag="mat%d" % n)
+            nc.vector.tensor_tensor(out=result[:], in0=acc[n][:], in1=fac_t[n][:], op=ALU.mult)
+            nc.sync.dma_start(out=out[P * n : P * (n + 1), :], in_=result[:])

@@ -26,10 +26,12 @@ PASSES = K // K_PASS
 TILES = H // P
 OUT_PASSES = H // K_PASS
 OUT_TILES = N // P
-HALF = S // 2
-CHUNKS = ((0, 1), (1, 1), (2, 2), (4, 2), (6, 2))
+CHUNKS = ((0, 1), (1, 1), (2, 1), (3, 1), (4, 2), (6, 2))
 VECTOR_COLS = 320
 PARKED = 6
+BY_PASS = 2
+LOOKS_BEFORE = {3: (0,), 4: (1, 2), 5: (3, 4), 6: (5,), 7: (6,)}
+ON_GPSIMD = (0,)
 
 
 def tile_list_lamp_service_scores_kernel(
@@ -56,22 +58,9 @@ def tile_list_lamp_service_scores_kernel(
         ident = new([P, P], F32, "ident")
         nc.vector.memset(tab_sc[:].bitcast(I32), 0)
         nc.vector.memset(wa_sc[:].bitcast(I32), 0)
-        nc.vector.memset(rows[:], 0.0)
         nc.vector.memset(wo_sc[:].bitcast(I32), 0)
+        nc.gpsimd.memset(rows[:], 0.0)
         make_identity(nc, ident[:])
-        for src, dst in ((tab_scales, tab_sc), (wa4_scales, wa_sc)):
-            for q in range(QUADS):
-                nc.gpsimd.dma_start(
-                    out=dst[QUAD * q : QUAD * q + 4].bitcast(I32),
-                    in_=src[:, 4 * q : 4 * q + 4, :].rearrange("a r t -> r a t").bitcast(I32),
-                )
-        for j, vec in enumerate((cap, thr, base)):
-            nc.gpsimd.dma_start(out=rows[TILES * j : TILES * (j + 1), :], in_=vec.rearrange("(c p) -> c p", p=P))
-        for q in range(QUADS):
-            nc.gpsimd.dma_start(
-                out=wo_sc[QUAD * q : QUAD * q + 4 * OUT_PASSES, :].bitcast(I32),
-                in_=wo8_scales[:, 4 * q : 4 * q + 4, :].bitcast(I32),
-            )
 
         tab = [new([P, T], U32, "tab%d" % a) for a in range(PASSES)]
         wa = [new([P, PASSES, H], U8, "wa%d" % b) for b in range(2)]
@@ -97,43 +86,62 @@ def tile_list_lamp_service_scores_kernel(
                     in_=wb[K_PASS * a : K_PASS * (a + 1), P * first : P * (first + count)].rearrange("(p j) c -> p j c", j=PACK),
                 )
 
+        def load_scales(dst, src):
+            for q in range(QUADS):
+                nc.sync.dma_start(
+                    out=dst[QUAD * q : QUAD * q + 4].bitcast(I32),
+                    in_=src[:, 4 * q : 4 * q + 4, :].rearrange("a r t -> r a t").bitcast(I32),
+                )
+
+        def load_tab(a):
+            nc.sync.dma_start(out=tab[a][:].bitcast(I32), in_=tab_words[a].rearrange("p t i -> p (t i)").bitcast(I32))
+
         def load_rows(tiles, src, c):
             nc.sync.dma_start(out=tiles[c][:], in_=src[P * c : P * (c + 1), :])
 
         nc.sync.dma_start(idx[:], offs)
-        for a in range(PASSES):
-            nc.sync.dma_start(out=tab[a][:].bitcast(I32), in_=tab_words[a].rearrange("p t i -> p (t i)").bitcast(I32))
+        for j, vec in enumerate((cap, thr, base)):
+            nc.sync.dma_start(out=rows[TILES * j : TILES * (j + 1), :], in_=vec.rearrange("(c p) -> c p", p=P))
+        load_tab(0)
+        load_scales(tab_sc, tab_scales)
+        load_tab(1)
         load_wa(0)
+        load_scales(wa_sc, wa4_scales)
+        load_tab(2)
         load_wb(0)
         load_rows(page, page0, 0)
         nc.sync.dma_start(out=wgs_t[:], in_=wgs)
         nc.sync.dma_start(idx2[:], offs2)
         load_wb(1)
+        load_wb(2)
         load_rows(page, page0, 1)
         nc.sync.dma_start(idx3[:], offs3)
-        load_wb(2)
-        load_rows(mat_t, mat, 0)
+        load_wb(3)
         load_rows(page, page0, 2)
-        load_rows(mat_t, mat, 1)
+        load_wb(4)
         load_rows(page, page0, 3)
         load_wa(1)
-        load_wb(3)
-        load_rows(mat_t, mat, 2)
         load_rows(page, page0, 4)
-        load_rows(mat_t, mat, 3)
+        load_rows(mat_t, mat, 0)
+        load_rows(mat_t, mat, 1)
+        load_wb(5)
         load_rows(page, page0, 5)
-        load_wb(4)
-        load_rows(mat_t, mat, 4)
+        load_rows(mat_t, mat, 2)
+        load_rows(mat_t, mat, 3)
         load_rows(page, page0, 6)
+        load_rows(page, page0, 7)
+        for c in range(4, TILES):
+            load_rows(mat_t, mat, c)
+        for q in range(QUADS):
+            nc.sync.dma_start(
+                out=wo_sc[QUAD * q : QUAD * q + 4 * OUT_PASSES, :].bitcast(I32),
+                in_=wo8_scales[:, 4 * q : 4 * q + 4, :].bitcast(I32),
+            )
         nc.sync.dma_start(out=wo[:].bitcast(I32), in_=wo8_words.rearrange("a p c i -> p a (c i)").bitcast(I32))
-        load_rows(mat_t, mat, 5)
         for n in range(OUT_TILES):
             load_rows(fac_t, fac, n)
-        load_rows(mat_t, mat, 6)
-        load_rows(mat_t, mat, 7)
-        load_rows(page, page0, 7)
 
-        turned = ps.tile([P, P], F32, name="turned", tag="out0")
+        turned = ps.tile([P, P], F32, name="turned", tag="bank7")
         nc.tensor.transpose(turned[:], rows[:], ident[:])
         cols = new([P, 3 * TILES], F32, "cols")
         nc.vector.tensor_copy(out=cols[:], in_=turned[:, : 3 * TILES])
@@ -148,32 +156,41 @@ def tile_list_lamp_service_scores_kernel(
         chunk_of = {first + i: (g, i) for g, (first, count) in enumerate(CHUNKS) for i in range(count)}
         grouped, wb_q, wb_sc, acc_a, plain, h, x, total, den, y = {}, {}, {}, {}, {}, {}, {}, {}, {}, {}
         parked = out.bitcast(BF16).rearrange("n (two m) -> (n two) m", two=2)
-        stage, y_q, y_sc, acc = {}, {}, {}, {}
+        stage, y_words, y_q, y_sc, acc = {}, {}, {}, {}, {}
 
         def interleave(copy, dst, src):
-            copy(out=dst.rearrange("p (c i) t -> p c t i", i=4), in_=src.rearrange("p t (c i) -> p c t i", i=4))
+            copy(out=dst, in_=src.rearrange("p t c -> p c t"))
 
         def round_wb(c):
             g, i = chunk_of[c]
             grouped[c] = new([P, PASSES, P, PACK], BF16, "grouped%d" % c)
             for a in range(PASSES):
-                interleave(nc.scalar.copy, grouped[c][:, a], raw[g, a][:, :, P * i : P * (i + 1)])
+                copy = nc.vector.tensor_copy if (c, a) == (0, PASSES - 1) else nc.scalar.copy
+                interleave(copy, grouped[c][:, a], raw[g, a][:, :, P * i : P * (i + 1)])
 
         def quantise_wb(c):
             wb_q[c] = new([P, PASSES * P], U32, "wb_q%d" % c)
             wb_sc[c] = new([P, PASSES * P], U8, "wb_sc%d" % c)
-            nc.vector.quantize_mx(
-                out=wb_q[c][:].bitcast(E4M3), scales=wb_sc[c][:], in_=grouped[c][:].rearrange("p a c t -> p (a c t)")
-            )
+            step = 1 if c < BY_PASS else PASSES
+            for a in range(0, PASSES, step):
+                part = slice(P * a, P * (a + step))
+                nc.vector.quantize_mx(
+                    out=wb_q[c][:, part].bitcast(E4M3), scales=wb_sc[c][:, part],
+                    in_=grouped[c][:, a : a + step].rearrange("p a c t -> p (a c t)"),
+                )
+
+        shared_home = {3: ("raw4_2", (0, 1, 2)), 5: ("raw5_2", (3, 4))}
+        plain_home = {0: "plain0", 1: "raw2_2", 2: "raw3_2", 4: "raw0_1", 6: "raw0_2", 7: "raw1_0"}
+        x_home = {5: "raw1_1", 6: "raw1_2", 7: "raw2_0"}
 
         def products(c):
-            acc_b = ps.tile([P, S], F32, name="acc_b%d" % c, tag="acc_b")
+            acc_b = ps.tile([P, S], F32, name="acc_b%d" % c, tag="bank%d" % (2 + c % 2))
             for a in range(PASSES):
                 nc.tensor.matmul_mx(
                     out=acc_b[:], lhsT=wb_q[c][:, P * a : P * (a + 1)].bitcast(E4M3), lhsT_scale=wb_sc[c][:, P * a : P * (a + 1)],
                     rhs=v[a][:].bitcast(E4M3), rhs_scale=v_sc[a][:], start=a == 0, stop=a == PASSES - 1,
                 )
-            acc_a[c] = ps.tile([P, S], F32, name="acc_a%d" % c, tag="acc_a")
+            acc_a[c] = ps.tile([P, S], F32, name="acc_a%d" % c, tag="bank%d" % (c % 2))
             b, i = divmod(c, PACK)
             for a in range(PASSES):
                 nc.tensor.matmul_mx(
@@ -181,71 +198,77 @@ def tile_list_lamp_service_scores_kernel(
                     lhsT_scale=wa_sc[:, a, P * c : P * (c + 1)],
                     rhs=v[a][:].bitcast(E4M3), rhs_scale=v_sc[a][:], start=a == 0, stop=a == PASSES - 1,
                 )
-            plain[c] = new([P, S], F32, "plain%d" % c, tag="plain%d" % (c % 2))
-            nc.scalar.copy(out=plain[c][:], in_=acc_b[:])
+            if c in shared_home:
+                tag, looks = shared_home[c]
+                shared = new([P, 1 + len(looks), S], F32, "shared%d" % c, tag=tag)
+                plain[c] = shared[:, 0, :]
+                for j, earlier in enumerate(looks):
+                    x[earlier] = shared[:, 1 + j, :]
+            else:
+                plain[c] = new([P, S], F32, "plain%d" % c, tag=plain_home[c])[:]
+            nc.scalar.copy(out=plain[c], in_=acc_b[:])
 
-        def put(c, half):
-            part = slice(HALF * half, HALF * (half + 1))
-            tag = "grouped%d" % (c + 1) if half == 1 and c + 1 < TILES else "h%d" % half
-            h[c, half] = (new([P, HALF], F32, "h%d_%d" % (c, half), tag=tag), tag)
+        def put(c):
+            h[c] = new([P, S], F32, "h%d" % c, tag="h%d" % (c % 2))
             nc.vector.scalar_tensor_tensor(
-                out=h[c, half][0][:], in0=acc_a[c][:, part], scalar=cols[:, c : c + 1], in1=plain[c][:, part],
-                op0=ALU.min, op1=ALU.add,
+                out=h[c][:], in0=acc_a[c][:], scalar=cols[:, c : c + 1], in1=plain[c], op0=ALU.min, op1=ALU.add
             )
-            entries = idx2[:, HALF // 16 * half : HALF // 16 * (half + 1)]
-            nc.vector.tensor_tensor(out=page[c][:].indirect(entries), in0=h[c, half][0][:], in1=wgs_t[:, part], op=ALU.mult)
-
-        x_home = ("raw2_2", "raw2_1", "raw3_2", "raw3_1", "raw4_2", "raw4_1", "raw0_2", "raw1_2")
+            nc.vector.tensor_tensor(out=page[c][:].indirect(idx2[:]), in0=h[c][:], in1=wgs_t[:], op=ALU.mult)
 
         def look(c):
-            x[c] = new([P, M], F32, "x%d" % c, tag=x_home[c])
-            total[c] = new([P, 1], F32, "total%d" % c)
+            if c in x_home:
+                x[c] = new([P, M], F32, "x%d" % c, tag=x_home[c])[:]
             den[c] = new([P, 1], F32, "den%d" % c)
+            base_col = cols[:, 2 * TILES + c : 2 * TILES + c + 1]
             nc.scalar.activation(
-                out=x[c][:], in_=page[c][:].indirect(idx3[:]), func=ACT.Sigmoid,
-                bias=cols[:, TILES + c : TILES + c + 1],
+                out=x[c], in_=page[c][:].indirect(idx3[:]), func=ACT.Sigmoid, bias=cols[:, TILES + c : TILES + c + 1]
             )
-            nc.scalar.activation(out=x[c][:], in_=x[c][:], func=ACT.Identity, accum_out=total[c][:])
-            nc.scalar.activation(
-                out=den[c][:], in_=total[c][:], func=ACT.Identity, bias=cols[:, 2 * TILES + c : 2 * TILES + c + 1]
-            )
+            if c == TILES - 1:
+                nc.vector.tensor_scalar(
+                    out=x[c], in0=x[c], scalar1=1.0, scalar2=base_col, op0=ALU.mult, op1=ALU.add, accum_out=den[c][:]
+                )
+            else:
+                total[c] = new([P, 1], F32, "total%d" % c)
+                nc.scalar.activation(out=x[c], in_=x[c], func=ACT.Identity, accum_out=total[c][:])
+                nc.scalar.activation(out=den[c][:], in_=total[c][:], func=ACT.Identity, bias=base_col)
 
         def weigh(c):
-            tag = h[c + 1, 1][1] if c + 1 < TILES else "rec_last"
-            rec = new([P, 1], F32, "rec%d" % c, tag=tag)
+            rec = new([P, 1], F32, "rec%d" % c)
             nc.vector.reciprocal(out=rec[:], in_=den[c][:])
-            y[c] = new([P, M], BF16, "y%d" % c, tag="y%d" % (c % 2))
+            y[c] = new([P, M], BF16, "y%d" % c)
             nc.vector.scalar_tensor_tensor(
-                out=y[c][:], in0=x[c][:], scalar=rec[:], in1=mat_t[c][:], op0=ALU.mult, op1=ALU.mult
+                out=y[c][:], in0=x[c], scalar=rec[:], in1=mat_t[c][:], op0=ALU.mult, op1=ALU.mult
             )
             b, q = divmod(c, QUADS)
-            if q == 0:
-                stage[b] = new([P, PACK, M], BF16, "stage%d" % b, tag=("raw2_0", "raw4_0")[b])
             if c >= PARKED:
                 for t in range(PACK):
                     nc.sync.dma_start(out=stage[b][QUAD * q : QUAD * (q + 1), t, :], in_=y[c][t:P:PACK, :])
             else:
-                nc.gpsimd.dma_start(out=parked[P * c : P * (c + 1), :], in_=y[c][:])
+                nc.scalar.dma_start(out=parked[P * c : P * (c + 1), :], in_=y[c][:])
                 if q == QUADS - 1 or c == PARKED - 1:
-                    nc.gpsimd.dma_start(
+                    stage[b] = new([P, PACK, M], BF16, "stage%d" % b, tag=("raw4_0", "raw5_0")[b])
+                    nc.scalar.dma_start(
                         out=stage[b][: QUAD * (q + 1)],
                         in_=parked[K_PASS * b : P * (c + 1), :].rearrange("(p t) m -> p t m", t=PACK),
                     )
 
-        def quantise_y(b):
-            words = new([P, M, PACK], BF16, "y_words%d" % b, tag=("raw3_0", "raw2_0")[b])
+        def regroup_y(b):
+            words = y_words[b] = new([P, M, PACK], BF16, "y_words%d" % b, tag=("raw4_1", "raw5_1")[b])
             if b == 0:
                 interleave(nc.scalar.copy, words[:], stage[b][:])
             else:
                 interleave(nc.vector.tensor_copy, words[:, :VECTOR_COLS], stage[b][:, :, :VECTOR_COLS])
                 interleave(nc.scalar.copy, words[:, VECTOR_COLS:], stage[b][:, :, VECTOR_COLS:])
-            y_q[b] = new([P, M], U32, "y_q%d" % b)
+
+        def quantise_y(b):
+            words = y_words[b]
+            y_q[b] = new([P, M], U32, "y_q%d" % b, tag=(x_home[TILES - 1], "y_q1")[b])
             y_sc[b] = new([P, M], U8, "y_sc%d" % b)
             nc.vector.quantize_mx(out=y_q[b][:].bitcast(E4M3), scales=y_sc[b][:], in_=words[:].rearrange("p m t -> p (m t)"))
 
         def scores(b, n):
             if b == 0:
-                acc[n] = ps.tile([P, M], F32, name="acc%d" % n, tag="out%d" % n)
+                acc[n] = ps.tile([P, M], F32, name="acc%d" % n, tag="bank%d" % (2 + n))
             nc.tensor.matmul_mx(
                 out=acc[n][:], lhsT=wo[:, b, P * n : P * (n + 1)].bitcast(E4M3), lhsT_scale=wo_sc[4 * b :, P * n : P * (n + 1)],
                 rhs=y_q[b][:].bitcast(E4M3), rhs_scale=y_sc[b][:], start=b == 0, stop=b == OUT_PASSES - 1,
@@ -254,28 +277,42 @@ def tile_list_lamp_service_scores_kernel(
         round_wb(0)
         quantise_wb(0)
         products(0)
+        put(0)
         round_wb(1)
-        for c in range(TILES):
-            put(c, 0)
-            if c + 1 < TILES:
-                quantise_wb(c + 1)
-            put(c, 1)
-            if c + 1 < TILES:
-                products(c + 1)
-            if c % 2 == 0 and c + 3 < TILES:
-                round_wb(c + 2)
-                round_wb(c + 3)
-            look(c)
-            if c >= 1:
-                weigh(c - 1)
-            if c == QUADS + 1:
-                quantise_y(0)
-                for n in range(OUT_TILES):
-                    scores(0, n)
+        quantise_wb(1)
+        for c in range(1, TILES):
+            first, count = CHUNKS[chunk_of[c + 1][0]] if c + 1 < TILES else (0, 0)
+            if first == c + 1:
+                for later in range(first, first + count):
+                    round_wb(later)
+                    quantise_wb(later)
+            products(c)
+            ready = LOOKS_BEFORE.get(c, ())
+            for earlier in ready:
+                look(earlier)
+            put(c)
+            for earlier in ready:
+                weigh(earlier)
+            if c == 5:
+                regroup_y(0)
+        look(TILES - 1)
         weigh(TILES - 1)
+        quantise_y(0)
+        for n in range(OUT_TILES):
+            scores(0, n)
+        regroup_y(1)
         quantise_y(1)
         for n in range(OUT_TILES):
             scores(1, n)
             result = new([P, M], F32, "result%d" % n, tag="mat%d" % n)
-            nc.vector.tensor_tensor(out=result[:], in0=acc[n][:], in1=fac_t[n][:], op=ALU.mult)
-            nc.sync.dma_start(out=out[P * n : P * (n + 1), :], in_=result[:])
+            if n in ON_GPSIMD:
+                sums = new([P, M], F32, "sums%d" % n, tag="h%d" % ON_GPSIMD.index(n))
+                nc.scalar.copy(out=sums[:], in_=acc[n][:])
+                nc.gpsimd.tensor_tensor(out=result[:], in0=sums[:], in1=fac_t[n][:], op=ALU.mult)
+                nc.sync.dma_start(out=out[P * n : P * (n + 1), :], in_=result[:])
+            else:
+                width = M // 2 if n == OUT_TILES - 1 else M
+                for m0 in range(0, M, width):
+                    part = slice(m0, m0 + width)
+                    nc.vector.tensor_tensor(out=result[:, part], in0=acc[n][:, part], in1=fac_t[n][:, part], op=ALU.mult)
+                    nc.sync.dma_start(out=out[P * n : P * (n + 1), part], in_=result[:, part])

@@ -26,12 +26,10 @@ PASSES = K // K_PASS
 TILES = H // P
 OUT_PASSES = H // K_PASS
 OUT_TILES = N // P
-CHUNKS = ((0, 1), (1, 1), (2, 1), (3, 1), (4, 2), (6, 2))
-VECTOR_COLS = 320
-PARKED = 6
-BY_PASS = 2
-LOOKS_BEFORE = {3: (0,), 4: (1, 2), 5: (3, 4), 6: (5,), 7: (6,)}
-ON_GPSIMD = (0,)
+PAIR = 2
+CHUNKS = TILES // PAIR
+BLOCKS = M // P
+HALF = M // 2
 
 
 def tile_list_lamp_service_scores_kernel(
@@ -61,13 +59,15 @@ def tile_list_lamp_service_scores_kernel(
         nc.vector.memset(wo_sc[:].bitcast(I32), 0)
         nc.gpsimd.memset(rows[:], 0.0)
         make_identity(nc, ident[:])
+        ident_bf = new([P, P], BF16, "ident_bf")
+        make_identity(nc, ident_bf[:])
 
         tab = [new([P, T], U32, "tab%d" % a) for a in range(PASSES)]
         wa = [new([P, PASSES, H], U8, "wa%d" % b) for b in range(2)]
         raw = {}
         page = [new([P, T2], F32, "page%d" % c) for c in range(TILES)]
         mat_t = [new([P, M], F32, "mat%d" % c) for c in range(TILES)]
-        fac_t = [new([P, M], F32, "fac%d" % n) for n in range(OUT_TILES)]
+        fac_t = [new([P, PAIR, M], F32, "fac%d" % j) for j in range(OUT_TILES // PAIR)]
         wgs_t = new([P, S], F32, "wgs")
         wo = new([P, OUT_PASSES, N], U32, "wo")
 
@@ -77,13 +77,12 @@ def tile_list_lamp_service_scores_kernel(
                 in_=wa4_words[:, :, H * b : H * (b + 1)].rearrange("a p n -> p a n").bitcast(I32),
             )
 
-        def load_wb(g):
-            first, count = CHUNKS[g]
-            for a in range(PASSES):
-                raw[g, a] = new([P, PACK, P * count], F32, "raw%d_%d" % (g, a))
+        def load_wb(g, passes=range(PASSES)):
+            for a in passes:
+                raw[g, a] = new([P, PACK, P * PAIR], F32, "raw%d_%d" % (g, a))
                 nc.sync.dma_start(
                     out=raw[g, a][:],
-                    in_=wb[K_PASS * a : K_PASS * (a + 1), P * first : P * (first + count)].rearrange("(p j) c -> p j c", j=PACK),
+                    in_=wb[K_PASS * a : K_PASS * (a + 1), P * PAIR * g : P * PAIR * (g + 1)].rearrange("(p j) c -> p j c", j=PACK),
                 )
 
         def load_scales(dst, src):
@@ -100,97 +99,108 @@ def tile_list_lamp_service_scores_kernel(
             nc.sync.dma_start(out=tiles[c][:], in_=src[P * c : P * (c + 1), :])
 
         nc.sync.dma_start(idx[:], offs)
-        for j, vec in enumerate((cap, thr, base)):
-            nc.sync.dma_start(out=rows[TILES * j : TILES * (j + 1), :], in_=vec.rearrange("(c p) -> c p", p=P))
         load_tab(0)
         load_scales(tab_sc, tab_scales)
         load_tab(1)
         load_wa(0)
+        load_wb(0, (0,))
         load_scales(wa_sc, wa4_scales)
+        load_wb(0, (1,))
         load_tab(2)
-        load_wb(0)
+        for j, vec in enumerate((cap, thr, base)):
+            nc.sync.dma_start(out=rows[TILES * j : TILES * (j + 1), :], in_=vec.rearrange("(c p) -> c p", p=P))
+        load_wb(0, (2,))
         load_rows(page, page0, 0)
         nc.sync.dma_start(out=wgs_t[:], in_=wgs)
         nc.sync.dma_start(idx2[:], offs2)
         load_wb(1)
-        load_wb(2)
-        load_rows(page, page0, 1)
         nc.sync.dma_start(idx3[:], offs3)
-        load_wb(3)
-        load_rows(page, page0, 2)
-        load_wb(4)
-        load_rows(page, page0, 3)
-        load_wa(1)
-        load_rows(page, page0, 4)
+        load_rows(page, page0, 1)
         load_rows(mat_t, mat, 0)
+        load_wb(2, (0,))
+        load_rows(page, page0, 2)
+        load_wb(2, (1, 2))
+        load_wa(1)
+        load_rows(page, page0, 3)
         load_rows(mat_t, mat, 1)
-        load_wb(5)
-        load_rows(page, page0, 5)
+        load_wb(3, (0,))
         load_rows(mat_t, mat, 2)
+        load_wb(3, (1,))
+        load_rows(page, page0, 4)
+        load_wb(3, (2,))
+        load_rows(page, page0, 5)
         load_rows(mat_t, mat, 3)
+        load_rows(mat_t, mat, 4)
         load_rows(page, page0, 6)
-        load_rows(page, page0, 7)
-        for c in range(4, TILES):
-            load_rows(mat_t, mat, c)
         for q in range(QUADS):
             nc.sync.dma_start(
                 out=wo_sc[QUAD * q : QUAD * q + 4 * OUT_PASSES, :].bitcast(I32),
                 in_=wo8_scales[:, 4 * q : 4 * q + 4, :].bitcast(I32),
             )
         nc.sync.dma_start(out=wo[:].bitcast(I32), in_=wo8_words.rearrange("a p c i -> p a (c i)").bitcast(I32))
-        for n in range(OUT_TILES):
-            load_rows(fac_t, fac, n)
+        load_rows(page, page0, 7)
+        for c in range(5, TILES):
+            load_rows(mat_t, mat, c)
+        for j in range(OUT_TILES // PAIR):
+            nc.sync.dma_start(out=fac_t[j][:], in_=fac[P * PAIR * j : P * PAIR * (j + 1), :].rearrange("(i p) m -> p i m", p=P))
 
         turned = ps.tile([P, P], F32, name="turned", tag="bank7")
         nc.tensor.transpose(turned[:], rows[:], ident[:])
         cols = new([P, 3 * TILES], F32, "cols")
-        nc.vector.tensor_copy(out=cols[:], in_=turned[:, : 3 * TILES])
+        nc.scalar.copy(out=cols[:], in_=turned[:, : 3 * TILES])
 
         v_sc = [new([P, S], U8, "v_sc%d" % a) for a in range(PASSES)]
         v = [new([P, S], U32, "v%d" % a) for a in range(PASSES)]
         for a in range(PASSES):
-            nc.vector.tensor_copy(out=v_sc[a][:], in_=tab_sc[:, a, :].indirect(idx[:]))
-        for a in range(PASSES):
             nc.vector.tensor_copy(out=v[a][:], in_=tab[a][:].indirect(idx[:]))
+            nc.vector.tensor_copy(out=v_sc[a][:], in_=tab_sc[:, a, :].indirect(idx[:]))
 
-        chunk_of = {first + i: (g, i) for g, (first, count) in enumerate(CHUNKS) for i in range(count)}
-        grouped, wb_q, wb_sc, acc_a, plain, h, x, total, den, y = {}, {}, {}, {}, {}, {}, {}, {}, {}, {}
-        parked = out.bitcast(BF16).rearrange("n (two m) -> (n two) m", two=2)
-        stage, y_words, y_q, y_sc, acc = {}, {}, {}, {}, {}
+        grouped, wb_q, wb_sc, acc_a, plain, h, x, den, rec = {}, {}, {}, {}, {}, {}, {}, {}, {}
+        turned_y, acc = {}, {}
 
-        def interleave(copy, dst, src):
-            copy(out=dst, in_=src.rearrange("p t c -> p c t"))
+        def round_wb(copy, dst, c, a):
+            g, i = divmod(c, PAIR)
+            copy(
+                out=dst.rearrange("p (c i) t -> p c t i", i=4),
+                in_=raw[g, a][:, :, P * i : P * (i + 1)].rearrange("p t (c i) -> p c t i", i=4),
+            )
 
-        def round_wb(c):
-            g, i = chunk_of[c]
-            grouped[c] = new([P, PASSES, P, PACK], BF16, "grouped%d" % c)
+        def round_pair(g, tag):
+            row = new([P, PAIR * PASSES * K_PASS], BF16, "grouped%d" % g, tag=tag)
+            pair = row[:].rearrange("p (i a c t) -> p i a c t", i=PAIR, a=PASSES, t=PACK)
             for a in range(PASSES):
-                copy = nc.vector.tensor_copy if (c, a) == (0, PASSES - 1) else nc.scalar.copy
-                interleave(copy, grouped[c][:, a], raw[g, a][:, :, P * i : P * (i + 1)])
+                for i in range(PAIR):
+                    grouped[PAIR * g + i] = pair[:, i]
+                    round_wb(nc.scalar.copy, pair[:, i, a], PAIR * g + i, a)
 
-        def quantise_wb(c):
-            wb_q[c] = new([P, PASSES * P], U32, "wb_q%d" % c)
-            wb_sc[c] = new([P, PASSES * P], U8, "wb_sc%d" % c)
-            step = 1 if c < BY_PASS else PASSES
-            for a in range(0, PASSES, step):
-                part = slice(P * a, P * (a + step))
-                nc.vector.quantize_mx(
-                    out=wb_q[c][:, part].bitcast(E4M3), scales=wb_sc[c][:, part],
-                    in_=grouped[c][:, a : a + step].rearrange("p a c t -> p (a c t)"),
-                )
+        def quantise_wb(c, src=None, first=0):
+            src = grouped[c] if src is None else src
+            if first == 0:
+                wb_q[c] = new([P, PASSES * P], U32, "wb_q%d" % c)
+                wb_sc[c] = new([P, PASSES * P], U8, "wb_sc%d" % c)
+            part = slice(P * first, P * (first + src.shape[1]))
+            nc.vector.quantize_mx(
+                out=wb_q[c][:, part].bitcast(E4M3), scales=wb_sc[c][:, part], in_=src.rearrange("p a c t -> p (a c t)")
+            )
 
-        shared_home = {3: ("raw4_2", (0, 1, 2)), 5: ("raw5_2", (3, 4))}
-        plain_home = {0: "plain0", 1: "raw2_2", 2: "raw3_2", 4: "raw0_1", 6: "raw0_2", 7: "raw1_0"}
-        x_home = {5: "raw1_1", 6: "raw1_2", 7: "raw2_0"}
+        def first_pair():
+            for first, count in ((0, PASSES - 1), (PASSES - 1, 1)):
+                part = [new([P, count, P, PACK], BF16, "grouped_first%d_%d" % (c, first)) for c in range(PAIR)]
+                for a in range(count):
+                    for c in range(PAIR):
+                        copy = nc.vector.tensor_copy if (c, first) == (0, PASSES - 1) else nc.scalar.copy
+                        round_wb(copy, part[c][:, a], c, first + a)
+                for c in range(PAIR):
+                    quantise_wb(c, part[c][:], first)
 
         def products(c):
-            acc_b = ps.tile([P, S], F32, name="acc_b%d" % c, tag="bank%d" % (2 + c % 2))
+            acc_b = ps.tile([P, S], F32, name="acc_b%d" % c, tag="bank%d" % (3 + c % 3))
             for a in range(PASSES):
                 nc.tensor.matmul_mx(
                     out=acc_b[:], lhsT=wb_q[c][:, P * a : P * (a + 1)].bitcast(E4M3), lhsT_scale=wb_sc[c][:, P * a : P * (a + 1)],
                     rhs=v[a][:].bitcast(E4M3), rhs_scale=v_sc[a][:], start=a == 0, stop=a == PASSES - 1,
                 )
-            acc_a[c] = ps.tile([P, S], F32, name="acc_a%d" % c, tag="bank%d" % (c % 2))
+            acc_a[c] = ps.tile([P, S], F32, name="acc_a%d" % c, tag="bank%d" % (c % 3))
             b, i = divmod(c, PACK)
             for a in range(PASSES):
                 nc.tensor.matmul_mx(
@@ -198,121 +208,222 @@ def tile_list_lamp_service_scores_kernel(
                     lhsT_scale=wa_sc[:, a, P * c : P * (c + 1)],
                     rhs=v[a][:].bitcast(E4M3), rhs_scale=v_sc[a][:], start=a == 0, stop=a == PASSES - 1,
                 )
-            if c in shared_home:
-                tag, looks = shared_home[c]
-                shared = new([P, 1 + len(looks), S], F32, "shared%d" % c, tag=tag)
-                plain[c] = shared[:, 0, :]
-                for j, earlier in enumerate(looks):
-                    x[earlier] = shared[:, 1 + j, :]
-            else:
-                plain[c] = new([P, S], F32, "plain%d" % c, tag=plain_home[c])[:]
-            nc.scalar.copy(out=plain[c], in_=acc_b[:])
+            plain[c] = new([P, S], F32, "plain%d" % c)
+            nc.scalar.copy(out=plain[c][:], in_=acc_b[:])
+
+        def after(tag, name, joined=None, weighed=()):
+            home = new([P, S + 8], F32, name, tag=tag)
+            if joined is not None:
+                h[joined] = home[:, :S]
+            for j, c in enumerate(weighed):
+                rec[c] = home[:, S + j : S + j + 1]
+
+        def join(c):
+            nc.vector.scalar_tensor_tensor(
+                out=h[c], in0=acc_a[c][:], scalar=cols[:, c : c + 1], in1=plain[c][:], op0=ALU.min, op1=ALU.add
+            )
 
         def put(c):
-            h[c] = new([P, S], F32, "h%d" % c, tag="h%d" % (c % 2))
-            nc.vector.scalar_tensor_tensor(
-                out=h[c][:], in0=acc_a[c][:], scalar=cols[:, c : c + 1], in1=plain[c], op0=ALU.min, op1=ALU.add
-            )
-            nc.vector.tensor_tensor(out=page[c][:].indirect(idx2[:]), in0=h[c][:], in1=wgs_t[:], op=ALU.mult)
+            nc.vector.tensor_tensor(out=page[c][:].indirect(idx2[:]), in0=h[c], in1=wgs_t[:], op=ALU.mult)
+
+        def hold_x(tiles, tag):
+            home = new([P, len(tiles), M], F32, "x%d" % tiles[0], tag=tag)
+            for j, c in enumerate(tiles):
+                x[c] = home[:, j, :]
 
         def look(c):
-            if c in x_home:
-                x[c] = new([P, M], F32, "x%d" % c, tag=x_home[c])[:]
             den[c] = new([P, 1], F32, "den%d" % c)
-            base_col = cols[:, 2 * TILES + c : 2 * TILES + c + 1]
+            total = new([P, 1], F32, "total%d" % c)
             nc.scalar.activation(
                 out=x[c], in_=page[c][:].indirect(idx3[:]), func=ACT.Sigmoid, bias=cols[:, TILES + c : TILES + c + 1]
             )
-            if c == TILES - 1:
-                nc.vector.tensor_scalar(
-                    out=x[c], in0=x[c], scalar1=1.0, scalar2=base_col, op0=ALU.mult, op1=ALU.add, accum_out=den[c][:]
+            nc.scalar.activation(out=x[c], in_=x[c], func=ACT.Identity, accum_out=total[:])
+            nc.scalar.activation(
+                out=den[c][:], in_=total[:], func=ACT.Identity, bias=cols[:, 2 * TILES + c : 2 * TILES + c + 1]
+            )
+
+        def look_last(c):
+            so_far = cols[:, 2 * TILES + c : 2 * TILES + c + 1]
+            for half in range(2):
+                x[c, half] = new([P, HALF], F32, "x%d_%d" % (c, half))
+                entries = idx3[:, HALF // 16 * half : HALF // 16 * (half + 1)]
+                nc.scalar.activation(
+                    out=x[c, half][:], in_=page[c][:].indirect(entries), func=ACT.Sigmoid, bias=cols[:, TILES + c : TILES + c + 1]
                 )
+                den[c] = new([P, 1], F32, "den%d_%d" % (c, half))
+                nc.vector.tensor_scalar(
+                    out=x[c, half][:], in0=x[c, half][:], scalar1=1.0, scalar2=so_far, op0=ALU.mult, op1=ALU.add,
+                    accum_out=den[c][:],
+                )
+                so_far = den[c][:]
+
+        def invert(c):
+            nc.vector.reciprocal(out=rec[c], in_=den[c][:])
+
+        def turn(c, y, first, count, bank_tag, last_copy):
+            b, q = divmod(c, QUADS)
+            bank = ps.tile([P, count, P], BF16, name="turn%d_%d" % (c, first), tag=bank_tag)
+            for j in range(count):
+                nc.tensor.transpose(bank[:, j, :], y[:, P * j : P * (j + 1)], ident_bf[:])
+            pairs = bank[:].bitcast(F32).rearrange("p j (k u) -> p j u k", u=2)
+            if b == 0:
+                nc.scalar.copy(out=turned_y[0][:, :, :, QUAD * q : QUAD * (q + 1)], in_=pairs)
             else:
-                total[c] = new([P, 1], F32, "total%d" % c)
-                nc.scalar.activation(out=x[c], in_=x[c], func=ACT.Identity, accum_out=total[c][:])
-                nc.scalar.activation(out=den[c][:], in_=total[c][:], func=ACT.Identity, bias=base_col)
+                for j in range(0, count, 2):
+                    half = (first + j) // 2
+                    last_copy(out=turned_y[1, half][:, :, :, QUAD * q : QUAD * (q + 1)], in_=pairs[:, j : j + 2])
 
         def weigh(c):
-            rec = new([P, 1], F32, "rec%d" % c)
-            nc.vector.reciprocal(out=rec[:], in_=den[c][:])
-            y[c] = new([P, M], BF16, "y%d" % c)
+            if c == 0:
+                turned_y[0] = new([P, BLOCKS, 2, P], F32, "turned_y0", tag="raw0_0")
+            if c == QUADS:
+                for half in range(2):
+                    turned_y[1, half] = new([P, 2, 2, P], F32, "turned_y1_%d" % half, tag=("raw0_1", "raw2_0")[half])
+            y = new([P, M], BF16, "y%d" % c)
+            nc.vector.scalar_tensor_tensor(out=y[:], in0=x[c], scalar=rec[c], in1=mat_t[c][:], op0=ALU.mult, op1=ALU.mult)
+            turn(c, y, 0, BLOCKS, "bank%d" % (6 + c % 2), nc.scalar.copy)
+
+        def weigh_last(c, half):
+            y = new([P, HALF], BF16, "y%d_%d" % (c, half))
             nc.vector.scalar_tensor_tensor(
-                out=y[c][:], in0=x[c], scalar=rec[:], in1=mat_t[c][:], op0=ALU.mult, op1=ALU.mult
+                out=y[:], in0=x[c, half][:], scalar=rec[c], in1=mat_t[c][:, HALF * half : HALF * (half + 1)],
+                op0=ALU.mult, op1=ALU.mult,
             )
-            b, q = divmod(c, QUADS)
-            if c >= PARKED:
-                for t in range(PACK):
-                    nc.sync.dma_start(out=stage[b][QUAD * q : QUAD * (q + 1), t, :], in_=y[c][t:P:PACK, :])
-            else:
-                nc.scalar.dma_start(out=parked[P * c : P * (c + 1), :], in_=y[c][:])
-                if q == QUADS - 1 or c == PARKED - 1:
-                    stage[b] = new([P, PACK, M], BF16, "stage%d" % b, tag=("raw4_0", "raw5_0")[b])
-                    nc.scalar.dma_start(
-                        out=stage[b][: QUAD * (q + 1)],
-                        in_=parked[K_PASS * b : P * (c + 1), :].rearrange("(p t) m -> p t m", t=PACK),
-                    )
+            turn(c, y, 2 * half, 2, "bank%d" % (7 - half), (nc.scalar.copy, nc.vector.tensor_copy)[half])
 
-        def regroup_y(b):
-            words = y_words[b] = new([P, M, PACK], BF16, "y_words%d" % b, tag=("raw4_1", "raw5_1")[b])
+        def turn_back(src, dst, b, half):
+            bank = ps.tile([P, 2, 2, P], F32, name="back%d_%d" % (b, half), tag="bank%d" % (7 - half))
+            for j in range(2):
+                for u in range(2):
+                    nc.tensor.transpose(bank[:, j, u, :], src[:, j, u, :], ident[:])
+            nc.scalar.copy(out=dst.bitcast(F32).rearrange("p (j m) u -> p j m u", m=P), in_=bank[:].rearrange("p j u m -> p j m u"))
+
+        def quantise_y(words, name, tag):
+            width = words.shape[1]
+            codes = new([P, width], U32, name + "_q", tag=tag)
+            scales = new([P, width], U8, name + "_sc")
+            nc.vector.quantize_mx(out=codes[:].bitcast(E4M3), scales=scales[:], in_=words.rearrange("p m t -> p (m t)"))
+            return codes, scales
+
+        def scores(b, half, j, codes, scales):
             if b == 0:
-                interleave(nc.scalar.copy, words[:], stage[b][:])
+                acc[half, j] = ps.tile([P, PAIR, HALF], F32, name="acc%d_%d" % (half, j), tag="bank%d" % (3 * half + j))
+            for i in range(PAIR):
+                n = PAIR * j + i
+                nc.tensor.matmul_mx(
+                    out=acc[half, j][:, i, :], lhsT=wo[:, b, P * n : P * (n + 1)].bitcast(E4M3),
+                    lhsT_scale=wo_sc[4 * b :, P * n : P * (n + 1)], rhs=codes.bitcast(E4M3), rhs_scale=scales,
+                    start=(b, i) == (0, 0), stop=(b, i) == (OUT_PASSES - 1, PAIR - 1),
+                )
+
+        def finish(half, j):
+            part = slice(HALF * half, HALF * (half + 1))
+            result = new([P, PAIR, HALF], F32, "result%d_%d" % (half, j), tag="mat%d" % (3 * half + j))
+            rows_out = out[P * PAIR * j : P * PAIR * (j + 1), part].rearrange("(i p) m -> p i m", p=P)
+            if (half, j) == (1, OUT_TILES // PAIR - 1):
+                for i in range(PAIR):
+                    nc.vector.tensor_tensor(out=result[:, i], in0=acc[half, j][:, i], in1=fac_t[j][:, i, part], op=ALU.mult)
+                    nc.sync.dma_start(out=rows_out[:, i], in_=result[:, i])
             else:
-                interleave(nc.vector.tensor_copy, words[:, :VECTOR_COLS], stage[b][:, :, :VECTOR_COLS])
-                interleave(nc.scalar.copy, words[:, VECTOR_COLS:], stage[b][:, :, VECTOR_COLS:])
+                nc.vector.tensor_tensor(out=result[:], in0=acc[half, j][:], in1=fac_t[j][:, :, part], op=ALU.mult)
+                nc.sync.dma_start(out=rows_out, in_=result[:])
 
-        def quantise_y(b):
-            words = y_words[b]
-            y_q[b] = new([P, M], U32, "y_q%d" % b, tag=(x_home[TILES - 1], "y_q1")[b])
-            y_sc[b] = new([P, M], U8, "y_sc%d" % b)
-            nc.vector.quantize_mx(out=y_q[b][:].bitcast(E4M3), scales=y_sc[b][:], in_=words[:].rearrange("p m t -> p (m t)"))
-
-        def scores(b, n):
-            if b == 0:
-                acc[n] = ps.tile([P, M], F32, name="acc%d" % n, tag="bank%d" % (2 + n))
-            nc.tensor.matmul_mx(
-                out=acc[n][:], lhsT=wo[:, b, P * n : P * (n + 1)].bitcast(E4M3), lhsT_scale=wo_sc[4 * b :, P * n : P * (n + 1)],
-                rhs=y_q[b][:].bitcast(E4M3), rhs_scale=y_sc[b][:], start=b == 0, stop=b == OUT_PASSES - 1,
-            )
-
-        round_wb(0)
-        quantise_wb(0)
+        first_pair()
         products(0)
+        products(1)
+        after("h0", "h0", joined=0)
+        join(0)
         put(0)
-        round_wb(1)
-        quantise_wb(1)
-        for c in range(1, TILES):
-            first, count = CHUNKS[chunk_of[c + 1][0]] if c + 1 < TILES else (0, 0)
-            if first == c + 1:
-                for later in range(first, first + count):
-                    round_wb(later)
-                    quantise_wb(later)
-            products(c)
-            ready = LOOKS_BEFORE.get(c, ())
-            for earlier in ready:
-                look(earlier)
-            put(c)
-            for earlier in ready:
-                weigh(earlier)
-            if c == 5:
-                regroup_y(0)
-        look(TILES - 1)
-        weigh(TILES - 1)
-        quantise_y(0)
-        for n in range(OUT_TILES):
-            scores(0, n)
-        regroup_y(1)
-        quantise_y(1)
-        for n in range(OUT_TILES):
-            scores(1, n)
-            result = new([P, M], F32, "result%d" % n, tag="mat%d" % n)
-            if n in ON_GPSIMD:
-                sums = new([P, M], F32, "sums%d" % n, tag="h%d" % ON_GPSIMD.index(n))
-                nc.scalar.copy(out=sums[:], in_=acc[n][:])
-                nc.gpsimd.tensor_tensor(out=result[:], in0=sums[:], in1=fac_t[n][:], op=ALU.mult)
-                nc.sync.dma_start(out=out[P * n : P * (n + 1), :], in_=result[:])
-            else:
-                width = M // 2 if n == OUT_TILES - 1 else M
-                for m0 in range(0, M, width):
-                    part = slice(m0, m0 + width)
-                    nc.vector.tensor_tensor(out=result[:, part], in0=acc[n][:, part], in1=fac_t[n][:, part], op=ALU.mult)
-                    nc.sync.dma_start(out=out[P * n : P * (n + 1), part], in_=result[:, part])
+
+        round_pair(1, "plain0")
+        hold_x((0,), "raw1_2")
+        look(0)
+        quantise_wb(2)
+        quantise_wb(3)
+        after("plain0", "h1", joined=1)
+        join(1)
+        products(2)
+        products(3)
+        put(1)
+
+        after("plain0", "h2", joined=2, weighed=(0,))
+        invert(0)
+        join(2)
+        weigh(0)
+        round_pair(2, "total0")
+        put(2)
+
+        hold_x((1, 2), "raw2_2")
+        look(1)
+        look(2)
+        quantise_wb(4)
+        quantise_wb(5)
+        after("total0", "h3", joined=3)
+        join(3)
+        products(4)
+        products(5)
+        put(3)
+
+        after("total0", "h4", joined=4, weighed=(1, 2))
+        invert(1)
+        join(4)
+        weigh(1)
+        invert(2)
+        weigh(2)
+        round_pair(3, "total2")
+        put(4)
+
+        hold_x((3, 4), "raw3_2")
+        look(3)
+        look(4)
+        quantise_wb(6)
+        quantise_wb(7)
+        after("total2", "h5", joined=5)
+        join(5)
+        products(6)
+        products(7)
+        put(5)
+
+        hold_x((5,), "plain1")
+        look(5)
+        after("total2", "h6", joined=6, weighed=(3, 4))
+        invert(3)
+        join(6)
+        weigh(3)
+        words = new([P, M, PACK], BF16, "y_words0", tag="raw1_0")
+        for half in range(2):
+            turn_back(turned_y[0][:, 2 * half : 2 * half + 2], words[:, HALF * half : HALF * (half + 1)], 0, half)
+        invert(4)
+        weigh(4)
+        put(6)
+
+        after("total2", "rec5", weighed=(5,))
+        invert(5)
+        weigh(5)
+        codes, scales = quantise_y(words[:], "y0", "plain3")
+        after("raw1_0", "h7", joined=7)
+        join(7)
+        for half in range(2):
+            for j in range(OUT_TILES // PAIR):
+                part = slice(HALF * half, HALF * (half + 1))
+                scores(0, half, j, codes[:, part], scales[:, part])
+        hold_x((6,), "raw0_0")
+        look(6)
+        put(7)
+
+        after("raw1_0", "rec6", weighed=(6, 7))
+        invert(6)
+        weigh(6)
+        look_last(7)
+        invert(7)
+        for half in range(2):
+            weigh_last(7, half)
+        last = []
+        for half in range(2):
+            words = new([P, HALF, PACK], BF16, "y_words1_%d" % half, tag=("raw1_1", "raw2_1")[half])
+            turn_back(turned_y[1, half][:], words[:], 1, half)
+            last.append(quantise_y(words[:], "y1_%d" % half, ("plain5", "plain6")[half]))
+        for half in range(2):
+            for j in range(OUT_TILES // PAIR):
+                scores(1, half, j, last[half][0][:], last[half][1][:])
+                finish(half, j)

from contextlib import ExitStack

import concourse.mybir as mybir
from concourse.masks import make_identity

K, H, N, T, S, T2, M = 1536, 1024, 768, 2048, 512, 1024, 512
FLOPS = 2 * (2 * K * H * S + H * N * M)

F32 = mybir.dt.float32
BF16 = mybir.dt.bfloat16
I32 = mybir.dt.int32
U32 = mybir.dt.uint32
U16 = mybir.dt.uint16
U8 = mybir.dt.uint8
E4M3 = mybir.dt.float8_e4m3fn_x4
E2M1 = mybir.dt.float4_e2m1fn_x4
ALU = mybir.AluOpType
ACT = mybir.ActivationFunctionType

P = 128
PACK = 4
K_PASS = P * PACK
QUADS = 4
QUAD = P // QUADS
PASSES = K // K_PASS
TILES = H // P
OUT_PASSES = H // K_PASS
OUT_TILES = N // P
PAIR = 2
CHUNKS = TILES // PAIR
BLOCKS = M // P
HALF = M // 2


def tile_list_lamp_service_scores_kernel(
    tc, tab_words, tab_scales, offs, offs2, offs3, wa4_words, wa4_scales, wb, cap, page0, wgs, thr, base, mat,
    wo8_words, wo8_scales, fac, out,
):
    nc = tc.nc
    with ExitStack() as ctx:
        lists = ctx.enter_context(tc.tile_pool(name="lists", bufs=1))
        sb = ctx.enter_context(tc.tile_pool(name="sb", bufs=1))
        ps = ctx.enter_context(tc.psum_pool(name="ps", bufs=1))

        def new(shape, dtype, name, tag=None):
            return sb.tile(shape, dtype, name=name, tag=tag or name, align_bytes=64)

        idx = lists.tile([P, S // 16], U16, name="idx")
        idx2 = lists.tile([P, S // 16], U16, name="idx2")
        idx3 = lists.tile([P, M // 16], U16, name="idx3")

        tab_sc = new([P, PASSES, T], U8, "tab_sc")
        wa_sc = new([P, PASSES, H], U8, "wa_sc")
        wo_sc = new([P, N], U8, "wo_sc")
        rows = new([P, P], F32, "rows")
        ident = new([P, P], F32, "ident")
        nc.vector.memset(tab_sc[:].bitcast(I32), 0)
        nc.vector.memset(wa_sc[:].bitcast(I32), 0)
        nc.vector.memset(wo_sc[:].bitcast(I32), 0)
        nc.gpsimd.memset(rows[:], 0.0)
        make_identity(nc, ident[:])
        ident_bf = new([P, P], BF16, "ident_bf")
        make_identity(nc, ident_bf[:])

        tab = [new([P, T], U32, "tab%d" % a) for a in range(PASSES)]
        wa = [new([P, PASSES, H], U8, "wa%d" % b) for b in range(2)]
        raw = {}
        page = [new([P, T2], F32, "page%d" % c) for c in range(TILES)]
        mat_t = [new([P, M], F32, "mat%d" % c) for c in range(TILES)]
        fac_t = [new([P, PAIR, M], F32, "fac%d" % j) for j in range(OUT_TILES // PAIR)]
        wgs_t = new([P, S], F32, "wgs")
        wo = new([P, OUT_PASSES, N], U32, "wo")

        def load_wa(b):
            nc.sync.dma_start(
                out=wa[b][:].bitcast(I32),
                in_=wa4_words[:, :, H * b : H * (b + 1)].rearrange("a p n -> p a n").bitcast(I32),
            )

        def load_wb(g, passes=range(PASSES)):
            for a in passes:
                raw[g, a] = new([P, PACK, P * PAIR], F32, "raw%d_%d" % (g, a))
                nc.sync.dma_start(
                    out=raw[g, a][:],
                    in_=wb[K_PASS * a : K_PASS * (a + 1), P * PAIR * g : P * PAIR * (g + 1)].rearrange("(p j) c -> p j c", j=PACK),
                )

        def load_scales(dst, src):
            for q in range(QUADS):
                nc.sync.dma_start(
                    out=dst[QUAD * q : QUAD * q + 4].bitcast(I32),
                    in_=src[:, 4 * q : 4 * q + 4, :].rearrange("a r t -> r a t").bitcast(I32),
                )

        def load_tab(a):
            nc.sync.dma_start(out=tab[a][:].bitcast(I32), in_=tab_words[a].rearrange("p t i -> p (t i)").bitcast(I32))

        def load_rows(tiles, src, c):
            nc.sync.dma_start(out=tiles[c][:], in_=src[P * c : P * (c + 1), :])

        nc.sync.dma_start(idx[:], offs)
        load_tab(0)
        load_scales(tab_sc, tab_scales)
        load_tab(1)
        load_wa(0)
        load_wb(0, (0,))
        load_scales(wa_sc, wa4_scales)
        load_wb(0, (1,))
        load_tab(2)
        for j, vec in enumerate((cap, thr, base)):
            nc.sync.dma_start(out=rows[TILES * j : TILES * (j + 1), :], in_=vec.rearrange("(c p) -> c p", p=P))
        load_wb(0, (2,))
        load_rows(page, page0, 0)
        nc.sync.dma_start(out=wgs_t[:], in_=wgs)
        nc.sync.dma_start(idx2[:], offs2)
        load_wb(1)
        nc.sync.dma_start(idx3[:], offs3)
        load_rows(page, page0, 1)
        load_rows(mat_t, mat, 0)
        load_wb(2, (0,))
        load_rows(page, page0, 2)
        load_wb(2, (1, 2))
        load_wa(1)
        load_rows(page, page0, 3)
        load_rows(mat_t, mat, 1)
        load_wb(3, (0,))
        load_rows(mat_t, mat, 2)
        load_wb(3, (1,))
        load_rows(page, page0, 4)
        load_wb(3, (2,))
        load_rows(page, page0, 5)
        load_rows(mat_t, mat, 3)
        load_rows(mat_t, mat, 4)
        load_rows(page, page0, 6)
        for q in range(QUADS):
            nc.sync.dma_start(
                out=wo_sc[QUAD * q : QUAD * q + 4 * OUT_PASSES, :].bitcast(I32),
                in_=wo8_scales[:, 4 * q : 4 * q + 4, :].bitcast(I32),
            )
        nc.sync.dma_start(out=wo[:].bitcast(I32), in_=wo8_words.rearrange("a p c i -> p a (c i)").bitcast(I32))
        load_rows(page, page0, 7)
        for c in range(5, TILES):
            load_rows(mat_t, mat, c)
        for j in range(OUT_TILES // PAIR):
            nc.sync.dma_start(out=fac_t[j][:], in_=fac[P * PAIR * j : P * PAIR * (j + 1), :].rearrange("(i p) m -> p i m", p=P))

        turned = ps.tile([P, P], F32, name="turned", tag="bank7")
        nc.tensor.transpose(turned[:], rows[:], ident[:])
        cols = new([P, 3 * TILES], F32, "cols")
        nc.scalar.copy(out=cols[:], in_=turned[:, : 3 * TILES])

        v_sc = [new([P, S], U8, "v_sc%d" % a) for a in range(PASSES)]
        v = [new([P, S], U32, "v%d" % a) for a in range(PASSES)]
        for a in range(PASSES):
            nc.vector.tensor_copy(out=v[a][:], in_=tab[a][:].indirect(idx[:]))
            nc.vector.tensor_copy(out=v_sc[a][:], in_=tab_sc[:, a, :].indirect(idx[:]))

        grouped, wb_q, wb_sc, acc_a, plain, h, x, den, rec = {}, {}, {}, {}, {}, {}, {}, {}, {}
        turned_y, acc = {}, {}

        def round_wb(copy, dst, c, a):
            g, i = divmod(c, PAIR)
            copy(
                out=dst.rearrange("p (c i) t -> p c t i", i=4),
                in_=raw[g, a][:, :, P * i : P * (i + 1)].rearrange("p t (c i) -> p c t i", i=4),
            )

        def round_pair(g, tag):
            row = new([P, PAIR * PASSES * K_PASS], BF16, "grouped%d" % g, tag=tag)
            pair = row[:].rearrange("p (i a c t) -> p i a c t", i=PAIR, a=PASSES, t=PACK)
            for a in range(PASSES):
                for i in range(PAIR):
                    grouped[PAIR * g + i] = pair[:, i]
                    round_wb(nc.scalar.copy, pair[:, i, a], PAIR * g + i, a)

        def quantise_wb(c, src=None, first=0):
            src = grouped[c] if src is None else src
            if first == 0:
                wb_q[c] = new([P, PASSES * P], U32, "wb_q%d" % c)
                wb_sc[c] = new([P, PASSES * P], U8, "wb_sc%d" % c)
            part = slice(P * first, P * (first + src.shape[1]))
            nc.vector.quantize_mx(
                out=wb_q[c][:, part].bitcast(E4M3), scales=wb_sc[c][:, part], in_=src.rearrange("p a c t -> p (a c t)")
            )

        def first_pair():
            for first, count in ((0, PASSES - 1), (PASSES - 1, 1)):
                part = [new([P, count, P, PACK], BF16, "grouped_first%d_%d" % (c, first)) for c in range(PAIR)]
                for a in range(count):
                    for c in range(PAIR):
                        copy = nc.vector.tensor_copy if (c, first) == (0, PASSES - 1) else nc.scalar.copy
                        round_wb(copy, part[c][:, a], c, first + a)
                for c in range(PAIR):
                    quantise_wb(c, part[c][:], first)

        def products(c):
            acc_b = ps.tile([P, S], F32, name="acc_b%d" % c, tag="bank%d" % (3 + c % 3))
            for a in range(PASSES):
                nc.tensor.matmul_mx(
                    out=acc_b[:], lhsT=wb_q[c][:, P * a : P * (a + 1)].bitcast(E4M3), lhsT_scale=wb_sc[c][:, P * a : P * (a + 1)],
                    rhs=v[a][:].bitcast(E4M3), rhs_scale=v_sc[a][:], start=a == 0, stop=a == PASSES - 1,
                )
            acc_a[c] = ps.tile([P, S], F32, name="acc_a%d" % c, tag="bank%d" % (c % 3))
            b, i = divmod(c, PACK)
            for a in range(PASSES):
                nc.tensor.matmul_mx(
                    out=acc_a[c][:], lhsT=wa[b][:, a, 2 * P * i : 2 * P * (i + 1)].bitcast(E2M1),
                    lhsT_scale=wa_sc[:, a, P * c : P * (c + 1)],
                    rhs=v[a][:].bitcast(E4M3), rhs_scale=v_sc[a][:], start=a == 0, stop=a == PASSES - 1,
                )
            plain[c] = new([P, S], F32, "plain%d" % c)
            nc.scalar.copy(out=plain[c][:], in_=acc_b[:])

        def after(tag, name, joined=None, weighed=()):
            home = new([P, S + 8], F32, name, tag=tag)
            if joined is not None:
                h[joined] = home[:, :S]
            for j, c in enumerate(weighed):
                rec[c] = home[:, S + j : S + j + 1]

        def join(c):
            nc.vector.scalar_tensor_tensor(
                out=h[c], in0=acc_a[c][:], scalar=cols[:, c : c + 1], in1=plain[c][:], op0=ALU.min, op1=ALU.add
            )

        def put(c):
            nc.vector.tensor_tensor(out=page[c][:].indirect(idx2[:]), in0=h[c], in1=wgs_t[:], op=ALU.mult)

        def hold_x(tiles, tag):
            home = new([P, len(tiles), M], F32, "x%d" % tiles[0], tag=tag)
            for j, c in enumerate(tiles):
                x[c] = home[:, j, :]

        def look(c):
            den[c] = new([P, 1], F32, "den%d" % c)
            total = new([P, 1], F32, "total%d" % c)
            nc.scalar.activation(
                out=x[c], in_=page[c][:].indirect(idx3[:]), func=ACT.Sigmoid, bias=cols[:, TILES + c : TILES + c + 1]
            )
            nc.scalar.activation(out=x[c], in_=x[c], func=ACT.Identity, accum_out=total[:])
            nc.scalar.activation(
                out=den[c][:], in_=total[:], func=ACT.Identity, bias=cols[:, 2 * TILES + c : 2 * TILES + c + 1]
            )

        def look_last(c):
            so_far = cols[:, 2 * TILES + c : 2 * TILES + c + 1]
            for half in range(2):
                x[c, half] = new([P, HALF], F32, "x%d_%d" % (c, half))
                entries = idx3[:, HALF // 16 * half : HALF // 16 * (half + 1)]
                nc.scalar.activation(
                    out=x[c, half][:], in_=page[c][:].indirect(entries), func=ACT.Sigmoid, bias=cols[:, TILES + c : TILES + c + 1]
                )
                den[c] = new([P, 1], F32, "den%d_%d" % (c, half))
                nc.vector.tensor_scalar(
                    out=x[c, half][:], in0=x[c, half][:], scalar1=1.0, scalar2=so_far, op0=ALU.mult, op1=ALU.add,
                    accum_out=den[c][:],
                )
                so_far = den[c][:]

        def invert(c):
            nc.vector.reciprocal(out=rec[c], in_=den[c][:])

        def turn(c, y, first, count, bank_tag, last_copy):
            b, q = divmod(c, QUADS)
            bank = ps.tile([P, count, P], BF16, name="turn%d_%d" % (c, first), tag=bank_tag)
            for j in range(count):
                nc.tensor.transpose(bank[:, j, :], y[:, P * j : P * (j + 1)], ident_bf[:])
            pairs = bank[:].bitcast(F32).rearrange("p j (k u) -> p j u k", u=2)
            if b == 0:
                nc.scalar.copy(out=turned_y[0][:, :, :, QUAD * q : QUAD * (q + 1)], in_=pairs)
            else:
                for j in range(0, count, 2):
                    half = (first + j) // 2
                    last_copy(out=turned_y[1, half][:, :, :, QUAD * q : QUAD * (q + 1)], in_=pairs[:, j : j + 2])

        def weigh(c):
            if c == 0:
                turned_y[0] = new([P, BLOCKS, 2, P], F32, "turned_y0", tag="raw0_0")
            if c == QUADS:
                for half in range(2):
                    turned_y[1, half] = new([P, 2, 2, P], F32, "turned_y1_%d" % half, tag=("raw0_1", "raw2_0")[half])
            y = new([P, M], BF16, "y%d" % c)
            nc.vector.scalar_tensor_tensor(out=y[:], in0=x[c], scalar=rec[c], in1=mat_t[c][:], op0=ALU.mult, op1=ALU.mult)
            turn(c, y, 0, BLOCKS, "bank%d" % (6 + c % 2), nc.scalar.copy)

        def weigh_last(c, half):
            y = new([P, HALF], BF16, "y%d_%d" % (c, half))
            nc.vector.scalar_tensor_tensor(
                out=y[:], in0=x[c, half][:], scalar=rec[c], in1=mat_t[c][:, HALF * half : HALF * (half + 1)],
                op0=ALU.mult, op1=ALU.mult,
            )
            turn(c, y, 2 * half, 2, "bank%d" % (7 - half), (nc.scalar.copy, nc.vector.tensor_copy)[half])

        def turn_back(src, dst, b, half):
            bank = ps.tile([P, 2, 2, P], F32, name="back%d_%d" % (b, half), tag="bank%d" % (7 - half))
            for j in range(2):
                for u in range(2):
                    nc.tensor.transpose(bank[:, j, u, :], src[:, j, u, :], ident[:])
            nc.scalar.copy(out=dst.bitcast(F32).rearrange("p (j m) u -> p j m u", m=P), in_=bank[:].rearrange("p j u m -> p j m u"))

        def quantise_y(words, name, tag):
            width = words.shape[1]
            codes = new([P, width], U32, name + "_q", tag=tag)
            scales = new([P, width], U8, name + "_sc")
            nc.vector.quantize_mx(out=codes[:].bitcast(E4M3), scales=scales[:], in_=words.rearrange("p m t -> p (m t)"))
            return codes, scales

        def scores(b, half, j, codes, scales):
            if b == 0:
                acc[half, j] = ps.tile([P, PAIR, HALF], F32, name="acc%d_%d" % (half, j), tag="bank%d" % (3 * half + j))
            for i in range(PAIR):
                n = PAIR * j + i
                nc.tensor.matmul_mx(
                    out=acc[half, j][:, i, :], lhsT=wo[:, b, P * n : P * (n + 1)].bitcast(E4M3),
                    lhsT_scale=wo_sc[4 * b :, P * n : P * (n + 1)], rhs=codes.bitcast(E4M3), rhs_scale=scales,
                    start=(b, i) == (0, 0), stop=(b, i) == (OUT_PASSES - 1, PAIR - 1),
                )

        def finish(half, j):
            part = slice(HALF * half, HALF * (half + 1))
            result = new([P, PAIR, HALF], F32, "result%d_%d" % (half, j), tag="mat%d" % (3 * half + j))
            rows_out = out[P * PAIR * j : P * PAIR * (j + 1), part].rearrange("(i p) m -> p i m", p=P)
            if (half, j) == (1, OUT_TILES // PAIR - 1):
                for i in range(PAIR):
                    nc.vector.tensor_tensor(out=result[:, i], in0=acc[half, j][:, i], in1=fac_t[j][:, i, part], op=ALU.mult)
                    nc.sync.dma_start(out=rows_out[:, i], in_=result[:, i])
            else:
                nc.vector.tensor_tensor(out=result[:], in0=acc[half, j][:], in1=fac_t[j][:, :, part], op=ALU.mult)
                nc.sync.dma_start(out=rows_out, in_=result[:])

        first_pair()
        products(0)
        products(1)
        after("h0", "h0", joined=0)
        join(0)
        put(0)

        round_pair(1, "plain0")
        hold_x((0,), "raw1_2")
        look(0)
        quantise_wb(2)
        quantise_wb(3)
        after("plain0", "h1", joined=1)
        join(1)
        products(2)
        products(3)
        put(1)

        after("plain0", "h2", joined=2, weighed=(0,))
        invert(0)
        join(2)
        weigh(0)
        round_pair(2, "total0")
        put(2)

        hold_x((1, 2), "raw2_2")
        look(1)
        look(2)
        quantise_wb(4)
        quantise_wb(5)
        after("total0", "h3", joined=3)
        join(3)
        products(4)
        products(5)
        put(3)

        after("total0", "h4", joined=4, weighed=(1, 2))
        invert(1)
        join(4)
        weigh(1)
        invert(2)
        weigh(2)
        round_pair(3, "total2")
        put(4)

        hold_x((3, 4), "raw3_2")
        look(3)
        look(4)
        quantise_wb(6)
        quantise_wb(7)
        after("total2", "h5", joined=5)
        join(5)
        products(6)
        products(7)
        put(5)

        hold_x((5,), "plain1")
        look(5)
        after("total2", "h6", joined=6, weighed=(3, 4))
        invert(3)
        join(6)
        weigh(3)
        words = new([P, M, PACK], BF16, "y_words0", tag="raw1_0")
        for half in range(2):
            turn_back(turned_y[0][:, 2 * half : 2 * half + 2], words[:, HALF * half : HALF * (half + 1)], 0, half)
        invert(4)
        weigh(4)
        put(6)

        after("total2", "rec5", weighed=(5,))
        invert(5)
        weigh(5)
        codes, scales = quantise_y(words[:], "y0", "plain3")
        after("raw1_0", "h7", joined=7)
        join(7)
        for half in range(2):
            for j in range(OUT_TILES // PAIR):
                part = slice(HALF * half, HALF * (half + 1))
                scores(0, half, j, codes[:, part], scales[:, part])
        hold_x((6,), "raw0_0")
        look(6)
        put(7)

        after("raw1_0", "rec6", weighed=(6, 7))
        invert(6)
        weigh(6)
        look_last(7)
        invert(7)
        for half in range(2):
            weigh_last(7, half)
        last = []
        for half in range(2):
            words = new([P, HALF, PACK], BF16, "y_words1_%d" % half, tag=("raw1_1", "raw2_1")[half])
            turn_back(turned_y[1, half][:], words[:], 1, half)
            last.append(quantise_y(words[:], "y1_%d" % half, ("plain5", "plain6")[half]))
        for half in range(2):
            for j in range(OUT_TILES // PAIR):
                scores(1, half, j, last[half][0][:], last[half][1][:])
                finish(half, j)
